import numpy as np
import ml_dtypes


def mxq(x, axis, fmt="e4m3"):
    dtype, down = {"e4m3": (ml_dtypes.float8_e4m3fn, 7), "e5m2": (ml_dtypes.float8_e5m2, 14)}[fmt]
    v = np.moveaxis(np.asarray(x, np.float32).astype(ml_dtypes.bfloat16).astype(np.float64), axis, -1)
    blocks = v.reshape(v.shape[:-1] + (-1, 32))
    amax = np.abs(blocks).max(-1, keepdims=True)
    byte = np.maximum(np.where(amax > 0, np.frexp(amax)[1] - 1 + 127, 0) - down, 1)
    scale = np.exp2(byte - 127.0)
    codes = (blocks / scale).astype(np.float32).astype(dtype).astype(np.float64)
    return np.moveaxis((codes * scale).reshape(v.shape), -1, axis)


WIDE = False


def mx_kscale(k):
    if not WIDE:
        return np.ones(k)
    levels = np.array([10, -10, 5, -5, 0])
    if k % 512:
        return np.exp2(np.random.permutation(np.resize(levels, k // 32))).repeat(32)
    a = np.empty((k // 512, 16))
    for p in range(k // 512):
        a[p, :8] = np.random.permutation(np.resize(levels, 8))
        for g in range(8):
            far = levels[np.abs(levels - a[p, g]) >= 10]
            a[p, g + 8] = far[np.random.randint(len(far))]
    return np.exp2(a.ravel()).repeat(32)


def f64(x):
    return np.asarray(x).astype(np.float64)


def striped(idx):
    return np.tile(idx.reshape(-1, 16).T, (8, 1)).astype(np.uint16)


def unstriped(offs):
    return offs[:16].T.reshape(-1).astype(np.int64)


def striped8(idx):
    return np.concatenate([v.reshape(-1, 16).T for v in idx]).astype(np.uint16)


def unstriped8(offs):
    return np.stack([offs[16 * g:16 * g + 16].T.reshape(-1) for g in range(8)]).astype(np.int64)


E2M1 = np.array([0.0, 0.5, 1.0, 1.5, 2.0, 3.0, 4.0, 6.0, -0.0, -0.5, -1.0, -1.5, -2.0, -3.0, -4.0, -6.0])


def pack_weight(w, fmt):
    k, n = w.shape
    w = f64(np.asarray(w, np.float32).astype(ml_dtypes.bfloat16)).reshape(k // 32, 32, n)
    amax = np.abs(w).max(1)
    if fmt == "e4m3":
        byte = np.frexp(amax)[1] - 1 + 127 - 7
    else:
        mant, ex = np.frexp(amax / 6.0)
        byte = np.where(mant > 0.5, ex, ex - 1) + 127
    byte = np.clip(np.where(amax > 0, byte, 1), 1, 254)
    scaled = (w * np.exp2(127.0 - byte)[:, None, :]).reshape(k, n).astype(np.float32)
    by_word = np.ascontiguousarray(scaled.reshape(k // 512, 128, 4, n).transpose(0, 1, 3, 2))
    if fmt == "e4m3":
        words = by_word.astype(ml_dtypes.float8_e4m3fn).view(np.uint8)
    else:
        c = by_word.astype(ml_dtypes.float4_e2m1fn).view(np.uint8) & 0xF
        words = (c[..., 0::2] | (c[..., 1::2] << 4)).reshape(k // 512, 128, 2 * n)
    return np.ascontiguousarray(words), np.ascontiguousarray(byte.astype(np.uint8).reshape(k // 512, 16, n))


def unpack_weight(words, scales, fmt):
    g, _, n = scales.shape
    words = np.ascontiguousarray(words).reshape(g, 128, n, -1)
    if fmt == "e4m3":
        vals = words.view(ml_dtypes.float8_e4m3fn).astype(np.float64)
    else:
        nib = np.empty((g, 128, n, 4), np.uint8)
        nib[..., 0::2] = words & 0xF
        nib[..., 1::2] = words >> 4
        vals = E2M1[nib]
    vals = vals * np.repeat(np.exp2(scales.astype(np.float64) - 127.0), 8, axis=1)[..., None]
    return vals.transpose(0, 1, 3, 2).reshape(g * 512, n)


def pack_table(v):
    words, scales = pack_weight(v, "e4m3")
    return np.concatenate([words.reshape(words.shape[0], -1), scales.reshape(scales.shape[0], -1)], axis=1)


def unpack_table(tab):
    g, t = tab.shape[0], tab.shape[1] // 528
    return unpack_weight(tab[:, :512 * t].reshape(g, 128, t, 4), tab[:, 512 * t:].reshape(g, 16, t), "e4m3")


K, M, T, S = 2048, 1024, 1024, 512


def setup_inputs():
    n = np.random.standard_normal
    s = mx_kscale(K)[:, None]
    u = mx_kscale(512)[:, None]
    p_w4 = pack_weight(n((K, M)) / np.sqrt(K) / s, "e2m1")
    return {
        "tab": pack_table(n((K, T)) * s),
        "w4_words": p_w4[0],
        "w4_scales": p_w4[1],
        "down": (n((K, 512)) / np.sqrt(K) / s * u.T).astype(np.float32),
        "up": (0.5 * n((512, M)) / np.sqrt(512) / u).astype(np.float32),
        "wgo": np.repeat(np.random.uniform(0.5, 2.0, (8, S)), 16, axis=0).astype(np.float32),
        "offs": striped(np.random.permutation(T)[:S]),
        "offs2": striped8(np.stack([np.random.permutation(T)[:S] for _ in range(8)])),
    }


def reference(tab, w4_words, w4_scales, down, up, wgo, offs, offs2):
    tab_ = unpack_table(tab)[:, unstriped(offs)]
    w4_ = unpack_weight(w4_words, w4_scales, "e2m1")
    down_ = mxq(f64(down), 0, "e4m3")
    up_ = mxq(f64(up), 0, "e4m3")
    h_ = mxq(down_.T @ tab_, 0, "e4m3")
    y = w4_.T @ tab_ + up_.T @ h_
    place = unstriped8(offs2)[np.arange(M) % 128 // 16]
    out = np.zeros((M, T))
    out[np.arange(M)[:, None], place] = f64(wgo)[np.arange(M) % 128] * (y)
    return out

@@ -1,0 +1,240 @@
+from contextlib import ExitStack
+
+import concourse.mybir as mybir
+
+K, M, T, S, R = 2048, 1024, 1024, 512, 512
+FLOPS = 2 * S * (K * R + K * M + R * M)
+
+F32 = mybir.dt.float32
+BF16 = mybir.dt.bfloat16
+I32 = mybir.dt.int32
+U32 = mybir.dt.uint32
+U16 = mybir.dt.uint16
+U8 = mybir.dt.uint8
+FP8X4 = mybir.dt.float8_e4m3fn_x4
+FP4X4 = mybir.dt.float4_e2m1fn_x4
+MULT = mybir.AluOpType.mult
+
+P = 128
+PACK = 4
+K_PASS = P * PACK
+PASSES = K // K_PASS
+QUADS = 4
+ROW_TILES = M // P
+QUARTER = S // 4
+PAGES = 3
+EARLY = 2 * P
+WEIGHT_GROUPS = ((0, 1), (1, 2), (2, 4), (4, 6), (6, 8))
+
+
+def tile_list_tabhs_l_none_kernel(tc, tab, w4_words, w4_scales, down, up, wgo, offs, offs2, out):
+    nc = tc.nc
+    with ExitStack() as ctx:
+        keep = ctx.enter_context(tc.tile_pool(name="keep", bufs=1))
+        psum = ctx.enter_context(tc.psum_pool(name="psum", bufs=8))
+
+        def held(name, shape, dtype, tag=None):
+            return keep.tile(shape, dtype, name=name, tag=tag or name, align_bytes=64)
+
+        pick = keep.tile([P, S // 16], U16, name="pick")
+        place = keep.tile([P, S // 16], U16, name="place")
+
+        tab_scales = held("tab_scales", [P, T], U8)
+        w4_sc_first = held("w4_sc_first", [P, PASSES, EARLY], U8)
+        w4_sc_rest = held("w4_sc_rest", [P, PASSES, M - EARLY], U8)
+        v_planes = held("v_planes", [P, PASSES, S], U8)
+        pages = [held(f"page{i}", [P, T], F32) for i in range(PAGES)]
+        nc.gpsimd.memset(tab_scales[P // 2 : P, :].bitcast(I32), 0)
+        nc.gpsimd.memset(w4_sc_first[:].bitcast(I32), 0)
+        nc.vector.memset(w4_sc_rest[:].bitcast(I32), 0)
+        nc.vector.memset(v_planes[:].bitcast(I32), 0)
+        for page in pages:
+            nc.vector.memset(page[:], 0.0)
+
+        tab_scale_rows = tab[:, K_PASS * T :].rearrange("a (q t) -> q a t", t=T)
+        w4_scale_rows = w4_scales.rearrange("a q n -> q a n")
+        for quad in range(QUADS):
+            nc.gpsimd.dma_start(
+                w4_sc_first[32 * quad : 32 * quad + 4, :, :].bitcast(I32),
+                w4_scale_rows[4 * quad : 4 * quad + 4, :, 0:EARLY].bitcast(I32),
+            )
+
+        tab_words = [held(f"tab_words{a}", [P, T], I32) for a in range(PASSES)]
+        down_raw = [held(f"down_raw{a}", [P, PACK, R], F32) for a in range(PASSES - 1)]
+        down_last = [held(f"down_last{h}", [P, PACK, R // 2], F32) for h in range(2)]
+        wgo_sb = held("wgo_sb", [P, S], F32)
+        up_raw = [held(f"up_raw{lo}", [P, PACK, (hi - lo) * P], F32) for lo, hi in WEIGHT_GROUPS]
+        w4_sb = [held(f"w4_sb{lo}", [P, PASSES, 2 * (hi - lo) * P], U8) for lo, hi in WEIGHT_GROUPS]
+        down_rows = down.rearrange("(a p j) r -> a p j r", p=P, j=PACK)
+        up_rows = up.rearrange("(p j) n -> p j n", j=PACK)
+        w4_rows = w4_words.rearrange("a p c -> p a c")
+
+        def load_tab(a):
+            nc.sync.dma_start(tab_words[a][:], tab[a, 0 : K_PASS * T].rearrange("(p c) -> p c", p=P).bitcast(I32))
+
+        def load_weights(g):
+            lo, hi = WEIGHT_GROUPS[g]
+            nc.sync.dma_start(up_raw[g][:], up_rows[:, :, lo * P : hi * P])
+            nc.sync.dma_start(w4_sb[g][:].bitcast(I32), w4_rows[:, :, 2 * lo * P : 2 * hi * P].bitcast(I32))
+
+        nc.sync.dma_start(tab_scales[0 : P // 2, :].bitcast(I32), tab_scale_rows.bitcast(I32))
+        nc.sync.dma_start(pick[:], offs)
+        nc.sync.dma_start(down_raw[0][:], down_rows[0])
+        nc.sync.dma_start(down_raw[1][:], down_rows[1])
+        load_tab(0)
+        nc.sync.dma_start(down_raw[2][:], down_rows[2])
+        load_tab(1)
+        load_tab(2)
+        for h in range(2):
+            nc.sync.dma_start(down_last[h][:], down_rows[PASSES - 1][:, :, h * (R // 2) : (h + 1) * (R // 2)])
+        load_tab(3)
+        load_weights(0)
+        nc.sync.dma_start(place[:], offs2)
+        nc.sync.dma_start(wgo_sb[:], wgo)
+        load_weights(1)
+        for quad in range(QUADS):
+            nc.sync.dma_start(
+                w4_sc_rest[32 * quad : 32 * quad + 4, :, :].bitcast(I32),
+                w4_scale_rows[4 * quad : 4 * quad + 4, :, EARLY:M].bitcast(I32),
+            )
+        for g in range(2, len(WEIGHT_GROUPS)):
+            load_weights(g)
+
+        v_scales = held("v_scales", [P, S], U8)
+        nc.vector.tensor_copy(v_scales[:], tab_scales[:].indirect(pick[:]))
+        for quad in range(QUADS):
+            nc.gpsimd.dma_start(
+                v_planes[32 * quad : 32 * quad + 4, :, :].bitcast(I32),
+                v_scales[16 * quad : 16 * quad + 16, :].bitcast(I32),
+            )
+
+        v_words = [held(f"v_words{a}", [P, S], U32) for a in range(PASSES)]
+        down_bf = [held(f"down_bf{a}", [P, R * PACK], BF16) for a in range(PASSES)]
+        down_codes = [held(f"down_codes{a}", [P, R], U32) for a in range(PASSES)]
+        down_scales = [held(f"down_scales{a}", [P, R], U8) for a in range(PASSES)]
+        h_banks = [psum.tile([P, PACK, QUARTER], F32, name=f"h_bank{q}", tag="bank") for q in range(4)]
+
+        def deal(dst, src):
+            return dict(
+                out=dst.rearrange("p t m j -> p m j t"), in_=src.rearrange("p j (m t) -> p m j t", t=PACK)
+            )
+
+        def h_matmuls(a, q):
+            cols = slice(q * QUARTER, (q + 1) * QUARTER)
+            for t in range(PACK):
+                nc.tensor.matmul_mx(
+                    out=h_banks[q][:, t, :],
+                    lhsT=down_codes[a][:, t * P : (t + 1) * P].bitcast(FP8X4),
+                    lhsT_scale=down_scales[a][:, t * P : (t + 1) * P],
+                    rhs=v_words[a][:, cols].bitcast(FP8X4),
+                    rhs_scale=v_planes[:, a, cols],
+                    start=(a == 0 and t == 0),
+                    stop=(a == PASSES - 1 and t == PACK - 1),
+                )
+
+        for a in range(PASSES):
+            dealt = down_bf[a][:].rearrange("p (t m j) -> p t m j", t=PACK, j=PACK)
+            if a < PASSES - 1:
+                nc.scalar.copy(**deal(dealt, down_raw[a][:]))
+            else:
+                nc.scalar.copy(**deal(dealt[:, :, 0 : P // 2, :], down_last[0][:]))
+                nc.vector.tensor_copy(**deal(dealt[:, :, P // 2 : P, :], down_last[1][:]))
+            nc.vector.quantize_mx(out=down_codes[a][:].bitcast(FP8X4), scales=down_scales[a][:], in_=down_bf[a][:])
+            if a < PASSES - 1:
+                nc.vector.tensor_copy(v_words[a][:], tab_words[a][:].bitcast(U32).indirect(pick[:]))
+                for q in range(4):
+                    h_matmuls(a, q)
+
+        up_codes = [held(f"up_codes{lo}", [P, (hi - lo) * P], U32) for lo, hi in WEIGHT_GROUPS]
+        up_scales = [held(f"up_scales{lo}", [P, (hi - lo) * P], U8) for lo, hi in WEIGHT_GROUPS]
+
+        def quantise_up(g, tag, cast):
+            lo, hi = WEIGHT_GROUPS[g]
+            up_bf = held(f"up_bf{g}", [P, (hi - lo) * P * PACK], BF16, tag)
+            cast(
+                out=up_bf[:].rearrange("p (c i j) -> p c j i", i=4, j=PACK),
+                in_=up_raw[g][:].rearrange("p j (c i) -> p c j i", i=4),
+            )
+            nc.vector.quantize_mx(out=up_codes[g][:].bitcast(FP8X4), scales=up_scales[g][:], in_=up_bf[:])
+
+        h_codes = held("h_codes", [P, S], U32)
+        h_scales = held("h_scales", [P, S], U8)
+
+        def y_matmuls(bank, n, cols):
+            g = [i for i, (lo, hi) in enumerate(WEIGHT_GROUPS) if lo <= n < hi][0]
+            c = (n - WEIGHT_GROUPS[g][0]) * P
+            for a in reversed(range(PASSES)):
+                w4_plane = w4_sc_first[:, a, n * P : (n + 1) * P] if n * P < EARLY else w4_sc_rest[:, a, n * P - EARLY : (n + 1) * P - EARLY]
+                nc.tensor.matmul_mx(
+                    out=bank,
+                    lhsT=w4_sb[g][:, a, 2 * c : 2 * (c + P)].bitcast(FP4X4),
+                    lhsT_scale=w4_plane,
+                    rhs=v_words[a][:, cols].bitcast(FP8X4),
+                    rhs_scale=v_planes[:, a, cols],
+                    start=(a == PASSES - 1),
+                    stop=False,
+                )
+            nc.tensor.matmul_mx(
+                out=bank,
+                lhsT=up_codes[g][:, c : c + P].bitcast(FP8X4),
+                lhsT_scale=up_scales[g][:, c : c + P],
+                rhs=h_codes[:, cols].bitcast(FP8X4),
+                rhs_scale=h_scales[:, cols],
+                start=False,
+                stop=True,
+            )
+
+        last = PASSES - 1
+        for q in range(4):
+            cols = slice(q * QUARTER, (q + 1) * QUARTER)
+            entries = pick[:, q * QUARTER // 16 : (q + 1) * QUARTER // 16]
+            nc.vector.tensor_copy(v_words[last][:, cols], tab_words[last][:].bitcast(U32).indirect(entries))
+            h_matmuls(last, q)
+        quantise_up(0, f"tab_words{last}", nc.vector.tensor_copy)
+
+        def quantise_h(q):
+            cols = slice(q * QUARTER, (q + 1) * QUARTER)
+            h_bf = held(f"h_bf{q}", [P, QUARTER * PACK], BF16, f"turn{q}")
+            nc.scalar.copy(
+                out=h_bf[:].rearrange("p (s t) -> p s t", t=PACK), in_=h_banks[q][:].rearrange("p t s -> p s t")
+            )
+            nc.vector.quantize_mx(out=h_codes[:, cols].bitcast(FP8X4), scales=h_scales[:, cols], in_=h_bf[:])
+
+        def first_tile_part(q, tag):
+            cols = slice(q * QUARTER, (q + 1) * QUARTER)
+            bank = psum.tile([P, QUARTER], F32, name="y_bank", tag="bank")
+            y_matmuls(bank[:], 0, cols)
+            y_part = held(f"y_part{q}", [P, QUARTER], F32, tag)
+            nc.scalar.copy(out=y_part[:], in_=bank[:])
+            entries = place[:, q * QUARTER // 16 : (q + 1) * QUARTER // 16]
+            nc.vector.tensor_tensor(pages[0][:].indirect(entries), y_part[:], wgo_sb[:, cols], MULT)
+
+        def row_tile(n, tag):
+            bank = psum.tile([P, S], F32, name="y_bank", tag="bank")
+            y_matmuls(bank[:], n, slice(0, S))
+            y_sb = held(f"y_sb{n}", [P, S], F32, tag)
+            nc.scalar.copy(out=y_sb[:], in_=bank[:])
+            page = pages[n % PAGES]
+            nc.vector.tensor_tensor(page[:].indirect(place[:]), y_sb[:], wgo_sb[:], MULT)
+            nc.sync.dma_start(out[n * P : (n + 1) * P, :], page[:])
+
+        quantise_h(0)
+        first_tile_part(0, None)
+        quantise_h(1)
+        first_tile_part(1, None)
+        quantise_h(2)
+        quantise_h(3)
+        quantise_up(1, "turn2", nc.scalar.copy)
+        first_tile_part(2, "up_raw1")
+        first_tile_part(3, None)
+        nc.sync.dma_start(out[0:P, :], pages[0][:])
+        quantise_up(2, "y_part1", nc.scalar.copy)
+        row_tile(1, "up_raw2")
+        quantise_up(3, "y_part3", nc.scalar.copy)
+        row_tile(2, None)
+        row_tile(3, "up_raw4")
+        quantise_up(4, "up_raw2", nc.scalar.copy)
+        row_tile(4, None)
+        row_tile(5, "up_raw6")
+        row_tile(6, None)
+        row_tile(7, None)

@@ -24,6 +24,26 @@ ROW_TILES = M // P
 QUARTER = S // 4
 PAGES = 3
 EARLY = 2 * P
+SHIFT_ROWS = 112
+SPLIT = 104
+SHARED = {
+    "down_raw0": 0,
+    "up_raw0": 0,
+    "w4_sb0": 2048,
+    "wgo_sb": 3072,
+    "up_raw1": 5120,
+    "w4_sb1": 7168,
+    "down_raw1": 8192,
+    "up_raw2": 8192,
+    "w4_sb2": 12288,
+    "w4_sc_rest": 14336,
+    "down_raw2": 17408,
+    "up_raw4": 17408,
+    "w4_sb4": 21504,
+    "w4_sb6": 23552,
+    "down_last0": 25600,
+    "up_raw6": 25600,
+}
 WEIGHT_GROUPS = ((0, 1), (1, 2), (2, 4), (4, 6), (6, 8))
 
 
@@ -31,9 +51,12 @@ def tile_list_tabhs_l_none_kernel(tc, tab, w4_words, w4_scales, down, up, wgo, o
     nc = tc.nc
     with ExitStack() as ctx:
         keep = ctx.enter_context(tc.tile_pool(name="keep", bufs=1))
+        shared = ctx.enter_context(tc.tile_pool(name="shared", bufs=1))
         psum = ctx.enter_context(tc.psum_pool(name="psum", bufs=8))
 
         def held(name, shape, dtype, tag=None):
+            if (tag or name) in SHARED:
+                return shared.tile(shape, dtype, name=name, offset=SHARED[tag or name], align_bytes=64)
             return keep.tile(shape, dtype, name=name, tag=tag or name, align_bytes=64)
 
         pick = keep.tile([P, S // 16], U16, name="pick")
@@ -41,30 +64,21 @@ def tile_list_tabhs_l_none_kernel(tc, tab, w4_words, w4_scales, down, up, wgo, o
 
         tab_scales = held("tab_scales", [P, T], U8)
         w4_sc_first = held("w4_sc_first", [P, PASSES, EARLY], U8)
-        w4_sc_rest = held("w4_sc_rest", [P, PASSES, M - EARLY], U8)
-        v_planes = held("v_planes", [P, PASSES, S], U8)
+        shifted = [held(f"shifted{a}", [P, S], U8) for a in range(1, PASSES)]
         pages = [held(f"page{i}", [P, T], F32) for i in range(PAGES)]
-        nc.gpsimd.memset(tab_scales[P // 2 : P, :].bitcast(I32), 0)
-        nc.gpsimd.memset(w4_sc_first[:].bitcast(I32), 0)
-        nc.vector.memset(w4_sc_rest[:].bitcast(I32), 0)
-        nc.vector.memset(v_planes[:].bitcast(I32), 0)
+        nc.gpsimd.memset(tab_scales[:].bitcast(I32), 0)
+        nc.vector.memset(w4_sc_first[:].bitcast(I32), 0)
+        for plane in shifted:
+            nc.vector.memset(plane[:].bitcast(I32), 0)
         for page in pages:
             nc.vector.memset(page[:], 0.0)
 
-        tab_scale_rows = tab[:, K_PASS * T :].rearrange("a (q t) -> q a t", t=T)
+        tab_scale_rows = tab[:, K_PASS * T :].rearrange("a (q t) -> a q t", t=T)
         w4_scale_rows = w4_scales.rearrange("a q n -> q a n")
-        for quad in range(QUADS):
-            nc.gpsimd.dma_start(
-                w4_sc_first[32 * quad : 32 * quad + 4, :, :].bitcast(I32),
-                w4_scale_rows[4 * quad : 4 * quad + 4, :, 0:EARLY].bitcast(I32),
-            )
 
         tab_words = [held(f"tab_words{a}", [P, T], I32) for a in range(PASSES)]
         down_raw = [held(f"down_raw{a}", [P, PACK, R], F32) for a in range(PASSES - 1)]
         down_last = [held(f"down_last{h}", [P, PACK, R // 2], F32) for h in range(2)]
-        wgo_sb = held("wgo_sb", [P, S], F32)
-        up_raw = [held(f"up_raw{lo}", [P, PACK, (hi - lo) * P], F32) for lo, hi in WEIGHT_GROUPS]
-        w4_sb = [held(f"w4_sb{lo}", [P, PASSES, 2 * (hi - lo) * P], U8) for lo, hi in WEIGHT_GROUPS]
         down_rows = down.rearrange("(a p j) r -> a p j r", p=P, j=PACK)
         up_rows = up.rearrange("(p j) n -> p j n", j=PACK)
         w4_rows = w4_words.rearrange("a p c -> p a c")
@@ -72,41 +86,38 @@ def tile_list_tabhs_l_none_kernel(tc, tab, w4_words, w4_scales, down, up, wgo, o
         def load_tab(a):
             nc.sync.dma_start(tab_words[a][:], tab[a, 0 : K_PASS * T].rearrange("(p c) -> p c", p=P).bitcast(I32))
 
-        def load_weights(g):
-            lo, hi = WEIGHT_GROUPS[g]
-            nc.sync.dma_start(up_raw[g][:], up_rows[:, :, lo * P : hi * P])
-            nc.sync.dma_start(w4_sb[g][:].bitcast(I32), w4_rows[:, :, 2 * lo * P : 2 * hi * P].bitcast(I32))
+        def load_w4_scales(plane, cols):
+            for quad in range(QUADS):
+                nc.sync.dma_start(
+                    plane[32 * quad : 32 * quad + 4, :, :].bitcast(I32),
+                    w4_scale_rows[4 * quad : 4 * quad + 4, :, cols].bitcast(I32),
+                )
 
-        nc.sync.dma_start(tab_scales[0 : P // 2, :].bitcast(I32), tab_scale_rows.bitcast(I32))
         nc.sync.dma_start(pick[:], offs)
+        nc.sync.dma_start(place[:], offs2)
         nc.sync.dma_start(down_raw[0][:], down_rows[0])
+        for quad in range(QUADS):
+            nc.sync.dma_start(
+                tab_scales[32 * quad : 32 * quad + 16, :].bitcast(I32),
+                tab_scale_rows[:, 4 * quad : 4 * quad + 4, :].bitcast(I32),
+            )
         nc.sync.dma_start(down_raw[1][:], down_rows[1])
         load_tab(0)
         nc.sync.dma_start(down_raw[2][:], down_rows[2])
         load_tab(1)
+        load_w4_scales(w4_sc_first, slice(0, EARLY))
         load_tab(2)
         for h in range(2):
             nc.sync.dma_start(down_last[h][:], down_rows[PASSES - 1][:, :, h * (R // 2) : (h + 1) * (R // 2)])
         load_tab(3)
-        load_weights(0)
-        nc.sync.dma_start(place[:], offs2)
-        nc.sync.dma_start(wgo_sb[:], wgo)
-        load_weights(1)
-        for quad in range(QUADS):
-            nc.sync.dma_start(
-                w4_sc_rest[32 * quad : 32 * quad + 4, :, :].bitcast(I32),
-                w4_scale_rows[4 * quad : 4 * quad + 4, :, EARLY:M].bitcast(I32),
-            )
-        for g in range(2, len(WEIGHT_GROUPS)):
-            load_weights(g)
 
         v_scales = held("v_scales", [P, S], U8)
         nc.vector.tensor_copy(v_scales[:], tab_scales[:].indirect(pick[:]))
-        for quad in range(QUADS):
-            nc.gpsimd.dma_start(
-                v_planes[32 * quad : 32 * quad + 4, :, :].bitcast(I32),
-                v_scales[16 * quad : 16 * quad + 16, :].bitcast(I32),
+        for a in range(1, PASSES):
+            nc.sync.dma_start(
+                shifted[a - 1][0:SHIFT_ROWS, :].bitcast(I32), v_scales[4 * a : 4 * a + SHIFT_ROWS, :].bitcast(I32)
             )
+        v_planes = [v_scales] + shifted
 
         v_words = [held(f"v_words{a}", [P, S], U32) for a in range(PASSES)]
         down_bf = [held(f"down_bf{a}", [P, R * PACK], BF16) for a in range(PASSES)]
@@ -127,7 +138,7 @@ def tile_list_tabhs_l_none_kernel(tc, tab, w4_words, w4_scales, down, up, wgo, o
                     lhsT=down_codes[a][:, t * P : (t + 1) * P].bitcast(FP8X4),
                     lhsT_scale=down_scales[a][:, t * P : (t + 1) * P],
                     rhs=v_words[a][:, cols].bitcast(FP8X4),
-                    rhs_scale=v_planes[:, a, cols],
+                    rhs_scale=v_scales[4 * a : P, cols],
                     start=(a == 0 and t == 0),
                     stop=(a == PASSES - 1 and t == PACK - 1),
                 )
@@ -135,15 +146,36 @@ def tile_list_tabhs_l_none_kernel(tc, tab, w4_words, w4_scales, down, up, wgo, o
         for a in range(PASSES):
             dealt = down_bf[a][:].rearrange("p (t m j) -> p t m j", t=PACK, j=PACK)
             if a < PASSES - 1:
-                nc.scalar.copy(**deal(dealt, down_raw[a][:]))
+                cast = nc.vector.tensor_copy if a == 1 else nc.scalar.copy
+                cast(**deal(dealt, down_raw[a][:]))
             else:
                 nc.scalar.copy(**deal(dealt[:, :, 0 : P // 2, :], down_last[0][:]))
-                nc.vector.tensor_copy(**deal(dealt[:, :, P // 2 : P, :], down_last[1][:]))
+                nc.vector.tensor_copy(**deal(dealt[:, :, P // 2 : SPLIT, :], down_last[1][:, :, 0 : PACK * (SPLIT - P // 2)]))
+                nc.scalar.copy(**deal(dealt[:, :, SPLIT:P, :], down_last[1][:, :, PACK * (SPLIT - P // 2) : R // 2]))
             nc.vector.quantize_mx(out=down_codes[a][:].bitcast(FP8X4), scales=down_scales[a][:], in_=down_bf[a][:])
             if a < PASSES - 1:
                 nc.vector.tensor_copy(v_words[a][:], tab_words[a][:].bitcast(U32).indirect(pick[:]))
                 for q in range(4):
                     h_matmuls(a, q)
+
+        wgo_sb = held("wgo_sb", [P, S], F32)
+        up_raw = [held(f"up_raw{lo}", [P, PACK, (hi - lo) * P], F32) for lo, hi in WEIGHT_GROUPS]
+        w4_sb = [held(f"w4_sb{lo}", [P, PASSES, 2 * (hi - lo) * P], U8) for lo, hi in WEIGHT_GROUPS]
+        w4_sc_rest = held("w4_sc_rest", [P, PASSES, M - EARLY], U8)
+
+        def load_weights(g):
+            lo, hi = WEIGHT_GROUPS[g]
+            nc.sync.dma_start(up_raw[g][:], up_rows[:, :, lo * P : hi * P])
+            nc.sync.dma_start(w4_sb[g][:].bitcast(I32), w4_rows[:, :, 2 * lo * P : 2 * hi * P].bitcast(I32))
+
+        load_weights(0)
+        nc.sync.dma_start(wgo_sb[:], wgo)
+        load_weights(1)
+        load_weights(2)
+        nc.vector.memset(w4_sc_rest[:].bitcast(I32), 0)
+        load_w4_scales(w4_sc_rest, slice(EARLY, M))
+        load_weights(3)
+        load_weights(4)
 
         up_codes = [held(f"up_codes{lo}", [P, (hi - lo) * P], U32) for lo, hi in WEIGHT_GROUPS]
         up_scales = [held(f"up_scales{lo}", [P, (hi - lo) * P], U8) for lo, hi in WEIGHT_GROUPS]
@@ -170,7 +202,7 @@ def tile_list_tabhs_l_none_kernel(tc, tab, w4_words, w4_scales, down, up, wgo, o
                     lhsT=w4_sb[g][:, a, 2 * c : 2 * (c + P)].bitcast(FP4X4),
                     lhsT_scale=w4_plane,
                     rhs=v_words[a][:, cols].bitcast(FP8X4),
-                    rhs_scale=v_planes[:, a, cols],
+                    rhs_scale=v_planes[a][:, cols],
                     start=(a == PASSES - 1),
                     stop=False,
                 )

@@ -28,23 +28,29 @@ SHIFT_ROWS = 112
 SPLIT = 104
 SHARED = {
     "down_raw0": 0,
-    "up_raw0": 0,
     "w4_sb0": 2048,
-    "wgo_sb": 3072,
-    "up_raw1": 5120,
-    "w4_sb1": 7168,
+    "wgo_sb": 4096,
+    "up_raw1": 6144,
     "down_raw1": 8192,
     "up_raw2": 8192,
+    "up_raw3": 10240,
     "w4_sb2": 12288,
     "w4_sc_rest": 14336,
     "down_raw2": 17408,
     "up_raw4": 17408,
     "w4_sb4": 21504,
-    "w4_sb6": 23552,
     "down_last0": 25600,
     "up_raw6": 25600,
+    "down_last1": 35840,
+    "up_raw0": 39936,
+    "h_bf": 39936,
+    "up_codes0": 29696,
+    "up_codes1": 30720,
+    "up_codes2": 31744,
+    "up_codes3": 33792,
 }
-WEIGHT_GROUPS = ((0, 1), (1, 2), (2, 4), (4, 6), (6, 8))
+UP_GROUPS = ((0, 1), (1, 2), (2, 3), (3, 4), (4, 6), (6, 8))
+W4_GROUPS = ((0, 2), (2, 4), (4, 8))
 
 
 def tile_list_tabhs_l_none_kernel(tc, tab, w4_words, w4_scales, down, up, wgo, offs, offs2, out):
@@ -52,7 +58,7 @@ def tile_list_tabhs_l_none_kernel(tc, tab, w4_words, w4_scales, down, up, wgo, o
     with ExitStack() as ctx:
         keep = ctx.enter_context(tc.tile_pool(name="keep", bufs=1))
         shared = ctx.enter_context(tc.tile_pool(name="shared", bufs=1))
-        psum = ctx.enter_context(tc.psum_pool(name="psum", bufs=8))
+        psum = ctx.enter_context(tc.psum_pool(name="psum", bufs=4))
 
         def held(name, shape, dtype, tag=None):
             if (tag or name) in SHARED:
@@ -93,9 +99,9 @@ def tile_list_tabhs_l_none_kernel(tc, tab, w4_words, w4_scales, down, up, wgo, o
                     w4_scale_rows[4 * quad : 4 * quad + 4, :, cols].bitcast(I32),
                 )
 
+        nc.sync.dma_start(down_raw[0][:], down_rows[0])
         nc.sync.dma_start(pick[:], offs)
         nc.sync.dma_start(place[:], offs2)
-        nc.sync.dma_start(down_raw[0][:], down_rows[0])
         for quad in range(QUADS):
             nc.sync.dma_start(
                 tab_scales[32 * quad : 32 * quad + 16, :].bitcast(I32),
@@ -113,7 +119,7 @@ def tile_list_tabhs_l_none_kernel(tc, tab, w4_words, w4_scales, down, up, wgo, o
 
         v_scales = held("v_scales", [P, S], U8)
         nc.vector.tensor_copy(v_scales[:], tab_scales[:].indirect(pick[:]))
-        for a in range(1, PASSES):
+        for a in reversed(range(1, PASSES)):
             nc.sync.dma_start(
                 shifted[a - 1][0:SHIFT_ROWS, :].bitcast(I32), v_scales[4 * a : 4 * a + SHIFT_ROWS, :].bitcast(I32)
             )
@@ -159,29 +165,36 @@ def tile_list_tabhs_l_none_kernel(tc, tab, w4_words, w4_scales, down, up, wgo, o
                     h_matmuls(a, q)
 
         wgo_sb = held("wgo_sb", [P, S], F32)
-        up_raw = [held(f"up_raw{lo}", [P, PACK, (hi - lo) * P], F32) for lo, hi in WEIGHT_GROUPS]
-        w4_sb = [held(f"w4_sb{lo}", [P, PASSES, 2 * (hi - lo) * P], U8) for lo, hi in WEIGHT_GROUPS]
+        up_raw = [held(f"up_raw{lo}", [P, PACK, (hi - lo) * P], F32) for lo, hi in UP_GROUPS]
+        w4_sb = [held(f"w4_sb{lo}", [P, PASSES, 2 * (hi - lo) * P], U8) for lo, hi in W4_GROUPS]
         w4_sc_rest = held("w4_sc_rest", [P, PASSES, M - EARLY], U8)
 
-        def load_weights(g):
-            lo, hi = WEIGHT_GROUPS[g]
+        def load_up(g):
+            lo, hi = UP_GROUPS[g]
             nc.sync.dma_start(up_raw[g][:], up_rows[:, :, lo * P : hi * P])
+
+        def load_w4(g):
+            lo, hi = W4_GROUPS[g]
             nc.sync.dma_start(w4_sb[g][:].bitcast(I32), w4_rows[:, :, 2 * lo * P : 2 * hi * P].bitcast(I32))
 
-        load_weights(0)
+        load_up(0)
+        load_w4(0)
         nc.sync.dma_start(wgo_sb[:], wgo)
-        load_weights(1)
-        load_weights(2)
+        load_up(1)
+        load_up(2)
+        load_up(3)
         nc.vector.memset(w4_sc_rest[:].bitcast(I32), 0)
         load_w4_scales(w4_sc_rest, slice(EARLY, M))
-        load_weights(3)
-        load_weights(4)
+        load_w4(1)
+        load_up(4)
+        load_w4(2)
+        load_up(5)
 
-        up_codes = [held(f"up_codes{lo}", [P, (hi - lo) * P], U32) for lo, hi in WEIGHT_GROUPS]
-        up_scales = [held(f"up_scales{lo}", [P, (hi - lo) * P], U8) for lo, hi in WEIGHT_GROUPS]
+        up_codes = [held(f"up_codes{lo}", [P, (hi - lo) * P], U32) for lo, hi in UP_GROUPS]
+        up_scales = [held(f"up_scales{lo}", [P, (hi - lo) * P], U8) for lo, hi in UP_GROUPS]
 
         def quantise_up(g, tag, cast):
-            lo, hi = WEIGHT_GROUPS[g]
+            lo, hi = UP_GROUPS[g]
             up_bf = held(f"up_bf{g}", [P, (hi - lo) * P * PACK], BF16, tag)
             cast(
                 out=up_bf[:].rearrange("p (c i j) -> p c j i", i=4, j=PACK),
@@ -193,13 +206,15 @@ def tile_list_tabhs_l_none_kernel(tc, tab, w4_words, w4_scales, down, up, wgo, o
         h_scales = held("h_scales", [P, S], U8)
 
         def y_matmuls(bank, n, cols):
-            g = [i for i, (lo, hi) in enumerate(WEIGHT_GROUPS) if lo <= n < hi][0]
-            c = (n - WEIGHT_GROUPS[g][0]) * P
+            g = [i for i, (lo, hi) in enumerate(UP_GROUPS) if lo <= n < hi][0]
+            c = (n - UP_GROUPS[g][0]) * P
+            gw = [i for i, (lo, hi) in enumerate(W4_GROUPS) if lo <= n < hi][0]
+            cw = (n - W4_GROUPS[gw][0]) * P
             for a in reversed(range(PASSES)):
                 w4_plane = w4_sc_first[:, a, n * P : (n + 1) * P] if n * P < EARLY else w4_sc_rest[:, a, n * P - EARLY : (n + 1) * P - EARLY]
                 nc.tensor.matmul_mx(
                     out=bank,
-                    lhsT=w4_sb[g][:, a, 2 * c : 2 * (c + P)].bitcast(FP4X4),
+                    lhsT=w4_sb[gw][:, a, 2 * cw : 2 * (cw + P)].bitcast(FP4X4),
                     lhsT_scale=w4_plane,
                     rhs=v_words[a][:, cols].bitcast(FP8X4),
                     rhs_scale=v_planes[a][:, cols],
@@ -217,27 +232,30 @@ def tile_list_tabhs_l_none_kernel(tc, tab, w4_words, w4_scales, down, up, wgo, o
             )
 
         last = PASSES - 1
-        for q in range(4):
-            cols = slice(q * QUARTER, (q + 1) * QUARTER)
-            entries = pick[:, q * QUARTER // 16 : (q + 1) * QUARTER // 16]
+        for lo, hi in ((0, 1), (1, 2), (2, 4)):
+            cols = slice(lo * QUARTER, hi * QUARTER)
+            entries = pick[:, lo * QUARTER // 16 : hi * QUARTER // 16]
             nc.vector.tensor_copy(v_words[last][:, cols], tab_words[last][:].bitcast(U32).indirect(entries))
-            h_matmuls(last, q)
-        quantise_up(0, f"tab_words{last}", nc.vector.tensor_copy)
+            for q in range(lo, hi):
+                h_matmuls(last, q)
+        quantise_up(0, "down_last1", nc.scalar.copy)
+
+        h_all = held("h_bf", [P, S * PACK], BF16)
 
         def quantise_h(q):
             cols = slice(q * QUARTER, (q + 1) * QUARTER)
-            h_bf = held(f"h_bf{q}", [P, QUARTER * PACK], BF16, f"turn{q}")
+            h_bf = h_all[:, q * QUARTER * PACK : (q + 1) * QUARTER * PACK]
             nc.scalar.copy(
-                out=h_bf[:].rearrange("p (s t) -> p s t", t=PACK), in_=h_banks[q][:].rearrange("p t s -> p s t")
+                out=h_bf.rearrange("p (s t) -> p s t", t=PACK), in_=h_banks[q][:].rearrange("p t s -> p s t")
             )
-            nc.vector.quantize_mx(out=h_codes[:, cols].bitcast(FP8X4), scales=h_scales[:, cols], in_=h_bf[:])
+            nc.vector.quantize_mx(out=h_codes[:, cols].bitcast(FP8X4), scales=h_scales[:, cols], in_=h_bf)
 
-        def first_tile_part(q, tag):
+        def first_tile_part(q, tag, empty):
             cols = slice(q * QUARTER, (q + 1) * QUARTER)
             bank = psum.tile([P, QUARTER], F32, name="y_bank", tag="bank")
             y_matmuls(bank[:], 0, cols)
             y_part = held(f"y_part{q}", [P, QUARTER], F32, tag)
-            nc.scalar.copy(out=y_part[:], in_=bank[:])
+            empty(out=y_part[:], in_=bank[:])
             entries = place[:, q * QUARTER // 16 : (q + 1) * QUARTER // 16]
             nc.vector.tensor_tensor(pages[0][:].indirect(entries), y_part[:], wgo_sb[:, cols], MULT)
 
@@ -251,22 +269,23 @@ def tile_list_tabhs_l_none_kernel(tc, tab, w4_words, w4_scales, down, up, wgo, o
             nc.sync.dma_start(out[n * P : (n + 1) * P, :], page[:])
 
         quantise_h(0)
-        first_tile_part(0, None)
+        first_tile_part(0, None, nc.vector.tensor_copy)
         quantise_h(1)
-        first_tile_part(1, None)
+        first_tile_part(1, None, nc.scalar.copy)
         quantise_h(2)
         quantise_h(3)
-        quantise_up(1, "turn2", nc.scalar.copy)
-        first_tile_part(2, "up_raw1")
-        first_tile_part(3, None)
+        quantise_up(1, "y_part0", nc.scalar.copy)
+        first_tile_part(2, "up_raw1", nc.scalar.copy)
+        first_tile_part(3, None, nc.scalar.copy)
         nc.sync.dma_start(out[0:P, :], pages[0][:])
-        quantise_up(2, "y_part1", nc.scalar.copy)
+        quantise_up(2, "up_codes0", nc.scalar.copy)
         row_tile(1, "up_raw2")
-        quantise_up(3, "y_part3", nc.scalar.copy)
-        row_tile(2, None)
+        quantise_up(3, "up_codes1", nc.scalar.copy)
+        row_tile(2, "up_raw3")
+        quantise_up(4, "up_codes2", nc.scalar.copy)
         row_tile(3, "up_raw4")
-        quantise_up(4, "up_raw2", nc.scalar.copy)
         row_tile(4, None)
+        quantise_up(5, "up_codes3", nc.scalar.copy)
         row_tile(5, "up_raw6")
         row_tile(6, None)
         row_tile(7, None)

@@ -102,13 +102,13 @@ def tile_list_tabhs_l_none_kernel(tc, tab, w4_words, w4_scales, down, up, wgo, o
         nc.sync.dma_start(down_raw[0][:], down_rows[0])
         nc.sync.dma_start(pick[:], offs)
         nc.sync.dma_start(place[:], offs2)
+        load_tab(0)
         for quad in range(QUADS):
             nc.sync.dma_start(
                 tab_scales[32 * quad : 32 * quad + 16, :].bitcast(I32),
                 tab_scale_rows[:, 4 * quad : 4 * quad + 4, :].bitcast(I32),
             )
         nc.sync.dma_start(down_raw[1][:], down_rows[1])
-        load_tab(0)
         nc.sync.dma_start(down_raw[2][:], down_rows[2])
         load_tab(1)
         load_w4_scales(w4_sc_first, slice(0, EARLY))
@@ -151,9 +151,11 @@ def tile_list_tabhs_l_none_kernel(tc, tab, w4_words, w4_scales, down, up, wgo, o
 
         for a in range(PASSES):
             dealt = down_bf[a][:].rearrange("p (t m j) -> p t m j", t=PACK, j=PACK)
-            if a < PASSES - 1:
-                cast = nc.vector.tensor_copy if a == 1 else nc.scalar.copy
-                cast(**deal(dealt, down_raw[a][:]))
+            if a < PASSES - 2:
+                nc.scalar.copy(**deal(dealt, down_raw[a][:]))
+            elif a < PASSES - 1:
+                nc.scalar.copy(**deal(dealt[:, :, 0 : P // 2, :], down_raw[a][:, :, 0 : R // 2]))
+                nc.vector.tensor_copy(**deal(dealt[:, :, P // 2 : P, :], down_raw[a][:, :, R // 2 : R]))
             else:
                 nc.scalar.copy(**deal(dealt[:, :, 0 : P // 2, :], down_last[0][:]))
                 nc.vector.tensor_copy(**deal(dealt[:, :, P // 2 : SPLIT, :], down_last[1][:, :, 0 : PACK * (SPLIT - P // 2)]))

from contextlib import ExitStack

import concourse.mybir as mybir

K, M, T, S, R = 2048, 1024, 1024, 512, 512
FLOPS = 2 * S * (K * R + K * M + R * M)

F32 = mybir.dt.float32
BF16 = mybir.dt.bfloat16
I32 = mybir.dt.int32
U32 = mybir.dt.uint32
U16 = mybir.dt.uint16
U8 = mybir.dt.uint8
FP8X4 = mybir.dt.float8_e4m3fn_x4
FP4X4 = mybir.dt.float4_e2m1fn_x4
MULT = mybir.AluOpType.mult

P = 128
PACK = 4
K_PASS = P * PACK
PASSES = K // K_PASS
QUADS = 4
ROW_TILES = M // P
QUARTER = S // 4
PAGES = 3
EARLY = 2 * P
SHIFT_ROWS = 112
SPLIT = 104
SHARED = {
    "down_raw0": 0,
    "w4_sb0": 2048,
    "wgo_sb": 4096,
    "up_raw1": 6144,
    "down_raw1": 8192,
    "up_raw2": 8192,
    "up_raw3": 10240,
    "w4_sb2": 12288,
    "w4_sc_rest": 14336,
    "down_raw2": 17408,
    "up_raw4": 17408,
    "w4_sb4": 21504,
    "down_last0": 25600,
    "up_raw6": 25600,
    "down_last1": 35840,
    "up_raw0": 39936,
    "h_bf": 39936,
    "up_codes0": 29696,
    "up_codes1": 30720,
    "up_codes2": 31744,
    "up_codes3": 33792,
}
UP_GROUPS = ((0, 1), (1, 2), (2, 3), (3, 4), (4, 6), (6, 8))
W4_GROUPS = ((0, 2), (2, 4), (4, 8))


def tile_list_tabhs_l_none_kernel(tc, tab, w4_words, w4_scales, down, up, wgo, offs, offs2, out):
    nc = tc.nc
    with ExitStack() as ctx:
        keep = ctx.enter_context(tc.tile_pool(name="keep", bufs=1))
        shared = ctx.enter_context(tc.tile_pool(name="shared", bufs=1))
        psum = ctx.enter_context(tc.psum_pool(name="psum", bufs=4))

        def held(name, shape, dtype, tag=None):
            if (tag or name) in SHARED:
                return shared.tile(shape, dtype, name=name, offset=SHARED[tag or name], align_bytes=64)
            return keep.tile(shape, dtype, name=name, tag=tag or name, align_bytes=64)

        pick = keep.tile([P, S // 16], U16, name="pick")
        place = keep.tile([P, S // 16], U16, name="place")

        tab_scales = held("tab_scales", [P, T], U8)
        w4_sc_first = held("w4_sc_first", [P, PASSES, EARLY], U8)
        shifted = [held(f"shifted{a}", [P, S], U8) for a in range(1, PASSES)]
        pages = [held(f"page{i}", [P, T], F32) for i in range(PAGES)]
        nc.gpsimd.memset(tab_scales[:].bitcast(I32), 0)
        nc.vector.memset(w4_sc_first[:].bitcast(I32), 0)
        for plane in shifted:
            nc.vector.memset(plane[:].bitcast(I32), 0)
        for page in pages:
            nc.vector.memset(page[:], 0.0)

        tab_scale_rows = tab[:, K_PASS * T :].rearrange("a (q t) -> a q t", t=T)
        w4_scale_rows = w4_scales.rearrange("a q n -> q a n")

        tab_words = [held(f"tab_words{a}", [P, T], I32) for a in range(PASSES)]
        down_raw = [held(f"down_raw{a}", [P, PACK, R], F32) for a in range(PASSES - 1)]
        down_last = [held(f"down_last{h}", [P, PACK, R // 2], F32) for h in range(2)]
        down_rows = down.rearrange("(a p j) r -> a p j r", p=P, j=PACK)
        up_rows = up.rearrange("(p j) n -> p j n", j=PACK)
        w4_rows = w4_words.rearrange("a p c -> p a c")

        def load_tab(a):
            nc.sync.dma_start(tab_words[a][:], tab[a, 0 : K_PASS * T].rearrange("(p c) -> p c", p=P).bitcast(I32))

        def load_w4_scales(plane, cols):
            for quad in range(QUADS):
                nc.sync.dma_start(
                    plane[32 * quad : 32 * quad + 4, :, :].bitcast(I32),
                    w4_scale_rows[4 * quad : 4 * quad + 4, :, cols].bitcast(I32),
                )

        nc.sync.dma_start(down_raw[0][:], down_rows[0])
        nc.sync.dma_start(pick[:], offs)
        nc.sync.dma_start(place[:], offs2)
        load_tab(0)
        for quad in range(QUADS):
            nc.sync.dma_start(
                tab_scales[32 * quad : 32 * quad + 16, :].bitcast(I32),
                tab_scale_rows[:, 4 * quad : 4 * quad + 4, :].bitcast(I32),
            )
        nc.sync.dma_start(down_raw[1][:], down_rows[1])
        nc.sync.dma_start(down_raw[2][:], down_rows[2])
        load_tab(1)
        load_w4_scales(w4_sc_first, slice(0, EARLY))
        load_tab(2)
        for h in range(2):
            nc.sync.dma_start(down_last[h][:], down_rows[PASSES - 1][:, :, h * (R // 2) : (h + 1) * (R // 2)])
        load_tab(3)

        v_scales = held("v_scales", [P, S], U8)
        nc.vector.tensor_copy(v_scales[:], tab_scales[:].indirect(pick[:]))
        for a in reversed(range(1, PASSES)):
            nc.sync.dma_start(
                shifted[a - 1][0:SHIFT_ROWS, :].bitcast(I32), v_scales[4 * a : 4 * a + SHIFT_ROWS, :].bitcast(I32)
            )
        v_planes = [v_scales] + shifted

        v_words = [held(f"v_words{a}", [P, S], U32) for a in range(PASSES)]
        down_bf = [held(f"down_bf{a}", [P, R * PACK], BF16) for a in range(PASSES)]
        down_codes = [held(f"down_codes{a}", [P, R], U32) for a in range(PASSES)]
        down_scales = [held(f"down_scales{a}", [P, R], U8) for a in range(PASSES)]
        h_banks = [psum.tile([P, PACK, QUARTER], F32, name=f"h_bank{q}", tag="bank") for q in range(4)]

        def deal(dst, src):
            return dict(
                out=dst.rearrange("p t m j -> p m j t"), in_=src.rearrange("p j (m t) -> p m j t", t=PACK)
            )

        def h_matmuls(a, q):
            cols = slice(q * QUARTER, (q + 1) * QUARTER)
            for t in range(PACK):
                nc.tensor.matmul_mx(
                    out=h_banks[q][:, t, :],
                    lhsT=down_codes[a][:, t * P : (t + 1) * P].bitcast(FP8X4),
                    lhsT_scale=down_scales[a][:, t * P : (t + 1) * P],
                    rhs=v_words[a][:, cols].bitcast(FP8X4),
                    rhs_scale=v_scales[4 * a : P, cols],
                    start=(a == 0 and t == 0),
                    stop=(a == PASSES - 1 and t == PACK - 1),
                )

        for a in range(PASSES):
            dealt = down_bf[a][:].rearrange("p (t m j) -> p t m j", t=PACK, j=PACK)
            if a < PASSES - 2:
                nc.scalar.copy(**deal(dealt, down_raw[a][:]))
            elif a < PASSES - 1:
                nc.scalar.copy(**deal(dealt[:, :, 0 : P // 2, :], down_raw[a][:, :, 0 : R // 2]))
                nc.vector.tensor_copy(**deal(dealt[:, :, P // 2 : P, :], down_raw[a][:, :, R // 2 : R]))
            else:
                nc.scalar.copy(**deal(dealt[:, :, 0 : P // 2, :], down_last[0][:]))
                nc.vector.tensor_copy(**deal(dealt[:, :, P // 2 : SPLIT, :], down_last[1][:, :, 0 : PACK * (SPLIT - P // 2)]))
                nc.scalar.copy(**deal(dealt[:, :, SPLIT:P, :], down_last[1][:, :, PACK * (SPLIT - P // 2) : R // 2]))
            nc.vector.quantize_mx(out=down_codes[a][:].bitcast(FP8X4), scales=down_scales[a][:], in_=down_bf[a][:])
            if a < PASSES - 1:
                nc.vector.tensor_copy(v_words[a][:], tab_words[a][:].bitcast(U32).indirect(pick[:]))
                for q in range(4):
                    h_matmuls(a, q)

        wgo_sb = held("wgo_sb", [P, S], F32)
        up_raw = [held(f"up_raw{lo}", [P, PACK, (hi - lo) * P], F32) for lo, hi in UP_GROUPS]
        w4_sb = [held(f"w4_sb{lo}", [P, PASSES, 2 * (hi - lo) * P], U8) for lo, hi in W4_GROUPS]
        w4_sc_rest = held("w4_sc_rest", [P, PASSES, M - EARLY], U8)

        def load_up(g):
            lo, hi = UP_GROUPS[g]
            nc.sync.dma_start(up_raw[g][:], up_rows[:, :, lo * P : hi * P])

        def load_w4(g):
            lo, hi = W4_GROUPS[g]
            nc.sync.dma_start(w4_sb[g][:].bitcast(I32), w4_rows[:, :, 2 * lo * P : 2 * hi * P].bitcast(I32))

        load_up(0)
        load_w4(0)
        nc.sync.dma_start(wgo_sb[:], wgo)
        load_up(1)
        load_up(2)
        load_up(3)
        nc.vector.memset(w4_sc_rest[:].bitcast(I32), 0)
        load_w4_scales(w4_sc_rest, slice(EARLY, M))
        load_w4(1)
        load_up(4)
        load_w4(2)
        load_up(5)

        up_codes = [held(f"up_codes{lo}", [P, (hi - lo) * P], U32) for lo, hi in UP_GROUPS]
        up_scales = [held(f"up_scales{lo}", [P, (hi - lo) * P], U8) for lo, hi in UP_GROUPS]

        def quantise_up(g, tag, cast):
            lo, hi = UP_GROUPS[g]
            up_bf = held(f"up_bf{g}", [P, (hi - lo) * P * PACK], BF16, tag)
            cast(
                out=up_bf[:].rearrange("p (c i j) -> p c j i", i=4, j=PACK),
                in_=up_raw[g][:].rearrange("p j (c i) -> p c j i", i=4),
            )
            nc.vector.quantize_mx(out=up_codes[g][:].bitcast(FP8X4), scales=up_scales[g][:], in_=up_bf[:])

        h_codes = held("h_codes", [P, S], U32)
        h_scales = held("h_scales", [P, S], U8)

        def y_matmuls(bank, n, cols):
            g = [i for i, (lo, hi) in enumerate(UP_GROUPS) if lo <= n < hi][0]
            c = (n - UP_GROUPS[g][0]) * P
            gw = [i for i, (lo, hi) in enumerate(W4_GROUPS) if lo <= n < hi][0]
            cw = (n - W4_GROUPS[gw][0]) * P
            for a in reversed(range(PASSES)):
                w4_plane = w4_sc_first[:, a, n * P : (n + 1) * P] if n * P < EARLY else w4_sc_rest[:, a, n * P - EARLY : (n + 1) * P - EARLY]
                nc.tensor.matmul_mx(
                    out=bank,
                    lhsT=w4_sb[gw][:, a, 2 * cw : 2 * (cw + P)].bitcast(FP4X4),
                    lhsT_scale=w4_plane,
                    rhs=v_words[a][:, cols].bitcast(FP8X4),
                    rhs_scale=v_planes[a][:, cols],
                    start=(a == PASSES - 1),
                    stop=False,
                )
            nc.tensor.matmul_mx(
                out=bank,
                lhsT=up_codes[g][:, c : c + P].bitcast(FP8X4),
                lhsT_scale=up_scales[g][:, c : c + P],
                rhs=h_codes[:, cols].bitcast(FP8X4),
                rhs_scale=h_scales[:, cols],
                start=False,
                stop=True,
            )

        last = PASSES - 1
        for lo, hi in ((0, 1), (1, 2), (2, 4)):
            cols = slice(lo * QUARTER, hi * QUARTER)
            entries = pick[:, lo * QUARTER // 16 : hi * QUARTER // 16]
            nc.vector.tensor_copy(v_words[last][:, cols], tab_words[last][:].bitcast(U32).indirect(entries))
            for q in range(lo, hi):
                h_matmuls(last, q)
        quantise_up(0, "down_last1", nc.scalar.copy)

        h_all = held("h_bf", [P, S * PACK], BF16)

        def quantise_h(q):
            cols = slice(q * QUARTER, (q + 1) * QUARTER)
            h_bf = h_all[:, q * QUARTER * PACK : (q + 1) * QUARTER * PACK]
            nc.scalar.copy(
                out=h_bf.rearrange("p (s t) -> p s t", t=PACK), in_=h_banks[q][:].rearrange("p t s -> p s t")
            )
            nc.vector.quantize_mx(out=h_codes[:, cols].bitcast(FP8X4), scales=h_scales[:, cols], in_=h_bf)

        def first_tile_part(q, tag, empty):
            cols = slice(q * QUARTER, (q + 1) * QUARTER)
            bank = psum.tile([P, QUARTER], F32, name="y_bank", tag="bank")
            y_matmuls(bank[:], 0, cols)
            y_part = held(f"y_part{q}", [P, QUARTER], F32, tag)
            empty(out=y_part[:], in_=bank[:])
            entries = place[:, q * QUARTER // 16 : (q + 1) * QUARTER // 16]
            nc.vector.tensor_tensor(pages[0][:].indirect(entries), y_part[:], wgo_sb[:, cols], MULT)

        def row_tile(n, tag):
            bank = psum.tile([P, S], F32, name="y_bank", tag="bank")
            y_matmuls(bank[:], n, slice(0, S))
            y_sb = held(f"y_sb{n}", [P, S], F32, tag)
            nc.scalar.copy(out=y_sb[:], in_=bank[:])
            page = pages[n % PAGES]
            nc.vector.tensor_tensor(page[:].indirect(place[:]), y_sb[:], wgo_sb[:], MULT)
            nc.sync.dma_start(out[n * P : (n + 1) * P, :], page[:])

        quantise_h(0)
        first_tile_part(0, None, nc.vector.tensor_copy)
        quantise_h(1)
        first_tile_part(1, None, nc.scalar.copy)
        quantise_h(2)
        quantise_h(3)
        quantise_up(1, "y_part0", nc.scalar.copy)
        first_tile_part(2, "up_raw1", nc.scalar.copy)
        first_tile_part(3, None, nc.scalar.copy)
        nc.sync.dma_start(out[0:P, :], pages[0][:])
        quantise_up(2, "up_codes0", nc.scalar.copy)
        row_tile(1, "up_raw2")
        quantise_up(3, "up_codes1", nc.scalar.copy)
        row_tile(2, "up_raw3")
        quantise_up(4, "up_codes2", nc.scalar.copy)
        row_tile(3, "up_raw4")
        row_tile(4, None)
        quantise_up(5, "up_codes3", nc.scalar.copy)
        row_tile(5, "up_raw6")
        row_tile(6, None)
        row_tile(7, None)
